import numpy as np
import ml_dtypes


def mxq(x, axis, fmt="e4m3"):
    dtype, down = {"e4m3": (ml_dtypes.float8_e4m3fn, 7), "e5m2": (ml_dtypes.float8_e5m2, 14)}[fmt]
    v = np.moveaxis(np.asarray(x, np.float32).astype(ml_dtypes.bfloat16).astype(np.float64), axis, -1)
    blocks = v.reshape(v.shape[:-1] + (-1, 32))
    amax = np.abs(blocks).max(-1, keepdims=True)
    byte = np.maximum(np.where(amax > 0, np.frexp(amax)[1] - 1 + 127, 0) - down, 1)
    scale = np.exp2(byte - 127.0)
    codes = (blocks / scale).astype(np.float32).astype(dtype).astype(np.float64)
    return np.moveaxis((codes * scale).reshape(v.shape), -1, axis)


WIDE = False


def mx_kscale(k):
    if not WIDE:
        return np.ones(k)
    levels = np.array([10, -10, 5, -5, 0])
    if k % 512:
        return np.exp2(np.random.permutation(np.resize(levels, k // 32))).repeat(32)
    a = np.empty((k // 512, 16))
    for p in range(k // 512):
        a[p, :8] = np.random.permutation(np.resize(levels, 8))
        for g in range(8):
            far = levels[np.abs(levels - a[p, g]) >= 10]
            a[p, g + 8] = far[np.random.randint(len(far))]
    return np.exp2(a.ravel()).repeat(32)


def f64(x):
    return np.asarray(x).astype(np.float64)


def striped(idx):
    return np.tile(idx.reshape(-1, 16).T, (8, 1)).astype(np.uint16)


def unstriped(offs):
    return offs[:16].T.reshape(-1).astype(np.int64)


E2M1 = np.array([0.0, 0.5, 1.0, 1.5, 2.0, 3.0, 4.0, 6.0, -0.0, -0.5, -1.0, -1.5, -2.0, -3.0, -4.0, -6.0])


def pack_weight(w, fmt):
    k, n = w.shape
    w = f64(np.asarray(w, np.float32).astype(ml_dtypes.bfloat16)).reshape(k // 32, 32, n)
    amax = np.abs(w).max(1)
    if fmt == "e4m3":
        byte = np.frexp(amax)[1] - 1 + 127 - 7
    else:
        mant, ex = np.frexp(amax / 6.0)
        byte = np.where(mant > 0.5, ex, ex - 1) + 127
    byte = np.clip(np.where(amax > 0, byte, 1), 1, 254)
    scaled = (w * np.exp2(127.0 - byte)[:, None, :]).reshape(k, n).astype(np.float32)
    by_word = np.ascontiguousarray(scaled.reshape(k // 512, 128, 4, n).transpose(0, 1, 3, 2))
    if fmt == "e4m3":
        words = by_word.astype(ml_dtypes.float8_e4m3fn).view(np.uint8)
    else:
        c = by_word.astype(ml_dtypes.float4_e2m1fn).view(np.uint8) & 0xF
        words = (c[..., 0::2] | (c[..., 1::2] << 4)).reshape(k // 512, 128, 2 * n)
    return np.ascontiguousarray(words), np.ascontiguousarray(byte.astype(np.uint8).reshape(k // 512, 16, n))


def unpack_weight(words, scales, fmt):
    g, _, n = scales.shape
    words = np.ascontiguousarray(words).reshape(g, 128, n, -1)
    if fmt == "e4m3":
        vals = words.view(ml_dtypes.float8_e4m3fn).astype(np.float64)
    else:
        nib = np.empty((g, 128, n, 4), np.uint8)
        nib[..., 0::2] = words & 0xF
        nib[..., 1::2] = words >> 4
        vals = E2M1[nib]
    vals = vals * np.repeat(np.exp2(scales.astype(np.float64) - 127.0), 8, axis=1)[..., None]
    return vals.transpose(0, 1, 3, 2).reshape(g * 512, n)


def relu(v):
    return np.maximum(v, 0.0)


def d_relu(v):
    return (v > 0).astype(np.float64)


K, T, E, C, H, N = 384, 640, 2, 256, 1024, 2048


def by_expert(wq, xq):
    return np.concatenate([wq[e].T @ xq[:, e * C:(e + 1) * C] for e in range(E)], axis=1)


def setup_inputs():
    n = np.random.standard_normal
    s = mx_kscale(N)[:, None]
    u = mx_kscale(H)
    w2 = [pack_weight(m, "e2m1") for m in n((E, N, H)) / np.sqrt(N) / s[None] * u[None, None, :]]
    w1 = [pack_weight(m, "e2m1") for m in n((E, H, K)) / np.sqrt(H) / u[None, :, None]]
    w3 = [pack_weight(m, "e2m1") for m in n((E, H, K)) / np.sqrt(H) / u[None, :, None]]
    return {
        "dyT": (n((N, T)) * s).astype(np.float32),
        "a1": n((H, E * C)).astype(np.float32),
        "a3": n((H, E * C)).astype(np.float32),
        "w2_words": np.stack([m[0] for m in w2]),
        "w2_scales": np.stack([m[1] for m in w2]),
        "w1_words": np.stack([m[0] for m in w1]),
        "w1_scales": np.stack([m[1] for m in w1]),
        "w3_words": np.stack([m[0] for m in w3]),
        "w3_scales": np.stack([m[1] for m in w3]),
        "gate": np.tile(np.random.uniform(0.2, 1.0, E * C), (N, 1)).astype(np.float32),
        "offs": striped(np.random.permutation(T)[:E * C]),
    }


def reference(dyT, a1, a3, w2_words, w2_scales, w1_words, w1_scales, w3_words, w3_scales, gate, offs):
    idx = unstriped(offs)
    w2 = np.stack([unpack_weight(w2_words[e], w2_scales[e], "e2m1") for e in range(E)])
    w1 = np.stack([unpack_weight(w1_words[e], w1_scales[e], "e2m1") for e in range(E)])
    w3 = np.stack([unpack_weight(w3_words[e], w3_scales[e], "e2m1") for e in range(E)])
    gq = mxq(f64(gate) * f64(dyT)[:, idx], 0, "e4m3")
    dh = by_expert(w2, gq)
    da1 = dh * f64(a3) * d_relu(f64(a1))
    da3 = dh * relu(f64(a1))
    dx = by_expert(w1, mxq(da1, 0, "e4m3")) + by_expert(w3, mxq(da3, 0, "e4m3"))
    out = np.zeros((K, T))
    out[:, idx] = dx
    return out

@@ -1,0 +1,310 @@
+from contextlib import ExitStack
+
+import concourse.mybir as mybir
+from concourse.masks import make_identity
+
+E, C, T, K, H, N = 2, 256, 640, 384, 1024, 2048
+S = E * C
+P = 128
+NP = N // 512
+HP = H // 512
+KT = K // P
+AT = C // P
+
+FLOPS = 2 * S * N * H + 2 * 2 * S * H * K
+BYTES = 4 * (N * T + 2 * H * S + P * S + K * T) + E * (N * H + 2 * H * K) * 17 // 32 + 2 * S * 8
+
+F32 = mybir.dt.float32
+BF16 = mybir.dt.bfloat16
+I32 = mybir.dt.int32
+U32 = mybir.dt.uint32
+U16 = mybir.dt.uint16
+U8 = mybir.dt.uint8
+FP8X4 = mybir.dt.float8_e4m3fn_x4
+FP4X4 = mybir.dt.float4_e2m1fn_x4
+MULT = mybir.AluOpType.mult
+RELU = mybir.ActivationFunctionType.Relu
+SIGN = mybir.ActivationFunctionType.Sign
+
+
+def tile_moe_bdx_glu_relu_kernel(
+    tc, dyT, a1, a3, w2_words, w2_scales, w1_words, w1_scales, w3_words, w3_scales, gate, offs, out
+):
+    nc = tc.nc
+    with ExitStack() as ctx:
+        keep = ctx.enter_context(tc.tile_pool(name="keep", bufs=1))
+        dypool = ctx.enter_context(tc.tile_pool(name="dypool", bufs=10))
+        gpool = ctx.enter_context(tc.tile_pool(name="gpool", bufs=2))
+        dpool = ctx.enter_context(tc.tile_pool(name="dpool", bufs=3))
+        psum = ctx.enter_context(tc.psum_pool(name="psum", bufs=1))
+
+        offsets = keep.tile([P, S // 16], U16, name="offsets")
+        nc.sync.dma_start(offsets[:], offs)
+        gates = keep.tile([P, S], F32, name="gates")
+        nc.scalar.dma_start(gates[:], gate[0:P, :])
+
+        w2s = keep.tile([P, E * NP, H], U8, name="w2s", align_bytes=64)
+        nc.vector.memset(w2s[:].bitcast(I32), 0)
+        w13s = keep.tile([P, E * HP, 2, K], U8, name="w13s", align_bytes=64)
+        nc.vector.memset(w13s[:].bitcast(I32), 0)
+        ident = keep.tile([P, P], F32, name="ident")
+        make_identity(nc, ident[:])
+        outs = []
+        for kt in range(KT):
+            o = keep.tile([P, T], F32, name=f"out{kt}")
+            nc.gpsimd.memset(o[:], 0.0)
+            outs.append(o)
+
+        dy_rows = dyT.rearrange("(s p t) w -> s t p w", s=NP, p=P, t=4)
+        a1_rows = a1.rearrange("(s p t) j -> s p t j", s=HP, p=P, t=4)
+        a3_rows = a3.rearrange("(s p t) j -> s p t j", s=HP, p=P, t=4)
+        dy = {}
+        w2t = []
+        a1t = {}
+        mr = {}
+
+        def load_dy(s):
+            for t in range(4):
+                d = dypool.tile([P, T], F32, name="dy")
+                nc.sync.dma_start(d[:], dy_rows[s, t])
+                dy[s, t] = d
+
+        def load_w2(s):
+            w = keep.tile([P, E, 2 * H], U8, name=f"w2t{s}", align_bytes=64)
+            nc.sync.dma_start(w[:].bitcast(I32), w2_words.bitcast(I32).rearrange("e s p w -> s p e w")[s])
+            w2t.append(w)
+
+        def load_a(e, h):
+            j = slice(C * e, C * (e + 1))
+            t1 = keep.tile([P, 4, C], F32, name=f"a1t{e}{h}")
+            nc.sync.dma_start(t1[:], a1_rows[h][:, :, j])
+            a1t[e, h] = t1
+            t3 = keep.tile([P, 2, 4, C], F32, name=f"mr{e}{h}")
+            nc.sync.dma_start(t3[:, 0], a3_rows[h][:, :, j])
+            mr[e, h] = t3
+
+        load_dy(0)
+        load_w2(0)
+        w2s_rows = w2_scales.bitcast(I32).rearrange("e s f i -> f (e s) i")
+        for q in range(4):
+            nc.sync.dma_start(w2s[32 * q : 32 * q + 4].bitcast(I32), w2s_rows[4 * q : 4 * q + 4])
+        load_dy(1)
+        load_w2(1)
+        load_dy(2)
+        load_w2(2)
+        load_a(0, 0)
+        load_a(0, 1)
+        load_dy(3)
+        load_w2(3)
+        w13 = keep.tile([P, E * HP, 2, 2 * K], U8, name="w13", align_bytes=64)
+        for w, words in ((0, w1_words), (1, w3_words)):
+            nc.sync.dma_start(
+                w13[:, :, w].bitcast(I32), words.bitcast(I32).rearrange("e s p w -> p (e s) w")
+            )
+        for w, scales in ((0, w1_scales), (1, w3_scales)):
+            rows = scales.bitcast(I32).rearrange("e s f k -> f (e s) k")
+            for q in range(4):
+                nc.sync.dma_start(w13s[32 * q : 32 * q + 4, :, w].bitcast(I32), rows[4 * q : 4 * q + 4])
+
+        load_a(1, 0)
+        load_a(1, 1)
+
+        mask = keep.tile([P, HP, S, 4], BF16, name="mask")
+
+        def masks(h, e, half):
+            j = slice(P * half, P * half + P)
+            nc.scalar.activation(mr[e, h][:, 1, :, j], a1t[e, h][:, :, j], RELU)
+            nc.scalar.activation(
+                mask[:, h, C * e + P * half : C * e + P * half + P],
+                mr[e, h][:, 1, :, j].rearrange("p t j -> p j t"),
+                SIGN,
+            )
+
+        gc = []
+        gs = []
+        for s in range(NP):
+            c = keep.tile([P, S], U32, name=f"gc{s}", align_bytes=64)
+            z = keep.tile([P, S], U8, name=f"gs{s}", align_bytes=64)
+            gc.append(c)
+            gs.append(z)
+
+        g4 = {}
+        gb = {}
+
+        def gather(s, t, e):
+            if (s, e) not in g4:
+                n = S if e is None else C
+                g = gpool.tile([P, 4, n], F32, name="g4" if e is None else "g4e")
+                g4[s, e] = g
+            g = g4[s, e]
+            o = offsets[:] if e is None else offsets[:, C // 16 * e : C // 16 * (e + 1)]
+            j = gates[:] if e is None else gates[:, C * e : C * (e + 1)]
+            nc.vector.tensor_tensor(g[:, t, :], dy[s, t][:].indirect(o), j, MULT)
+
+        def interleave(s, e, a=0):
+            n = S if e is None else P
+            b = gpool.tile([P, n, 4], BF16, name="gb" if e is None else "gbe", align_bytes=64)
+            nc.scalar.copy(b[:], g4[s, e][:, :, n * a : n * (a + 1)].rearrange("p t j -> p j t"))
+            gb[s, e, a] = b
+
+        def quant_g(s, e, a=0):
+            j = slice(0, S) if e is None else slice(C * e + P * a, C * e + P * (a + 1))
+            nc.vector.quantize_mx(
+                out=gc[s][:, j].bitcast(FP8X4), scales=gs[s][:, j], in_=gb[s, e, a][:].rearrange("p j t -> p (j t)")
+            )
+
+        bank = {}
+
+        def mm1(s, e, some=range(AT)):
+            for a in some:
+                j = slice(C * e + P * a, C * e + P * a + P)
+                for h in range(HP):
+                    if s == 0:
+                        b = psum.tile([P, 512], F32, name=f"bank{e}{a}{h}")
+                        bank[e, a, h] = b
+                    nc.tensor.matmul_mx(
+                        out=bank[e, a, h][:],
+                        lhsT=gc[s][:, j].bitcast(FP8X4),
+                        lhsT_scale=gs[s][:, j],
+                        rhs=w2t[s][:, e, 1024 * h : 1024 * (h + 1)].bitcast(FP4X4),
+                        rhs_scale=w2s[:, e * NP + s, 512 * h : 512 * (h + 1)],
+                        start=(s == 0),
+                        stop=(s == NP - 1),
+                    )
+
+        def turn(e, a, h):
+            d = dpool.tile([P, 4, P], F32, name="dhs")
+            nc.scalar.copy(d[:], bank[e, a, h][:].rearrange("p (m t) -> p t m", t=4))
+            b = psum.tile([P, 4, P], F32, name=f"bank{e}{a}{h}")
+            for t in range(4):
+                nc.tensor.transpose(b[:, t, :], d[:, t, :], ident[:])
+            bank[e, a, h] = b
+
+        dq = {}
+
+        def products(e, a, h):
+            if h == 0:
+                q = dpool.tile([P, HP, 2, P, 4], BF16, name="dq", align_bytes=64)
+                dq[e, a] = q
+            j = slice(P * a, P * a + P)
+            nc.vector.tensor_tensor(
+                dq[e, a][:, h],
+                bank[e, a, h][:].rearrange("p t j -> p j t").unsqueeze(1).to_broadcast([P, 2, P, 4]),
+                mr[e, h][:, :, :, j].rearrange("p w t j -> p w j t"),
+                MULT,
+            )
+
+        def masked(e, a):
+            j = slice(C * e + P * a, C * e + P * a + P)
+            m = dq[e, a][:, :, 0]
+            nc.vector.tensor_tensor(m, m, mask[:, :, j], MULT)
+
+        dc = {}
+
+        def quant_d(e, a):
+            c = dpool.tile([P, HP * 2 * P], U32, name="dc", align_bytes=64)
+            z = dpool.tile([P, HP * 2 * P], U8, name="ds", align_bytes=64)
+            nc.vector.quantize_mx(
+                out=c[:].bitcast(FP8X4), scales=z[:], in_=dq[e, a][:].rearrange("p h w j t -> p (h w j t)")
+            )
+            dc[e, a] = (c, z)
+
+        dxs = []
+        for e in range(E):
+            d = keep.tile([P, KT, C], F32, name=f"dxs{e}")
+            dxs.append(d)
+
+        def mm2(e, a):
+            c, z = dc[e, a]
+            b = psum.tile([P, KT, P], F32, name=f"bank{e}{a}0")
+            for kt in range(KT):
+                for h in range(HP):
+                    for w in range(2):
+                        r = slice(P * (2 * h + w), P * (2 * h + w + 1))
+                        nc.tensor.matmul_mx(
+                            out=b[:, kt],
+                            lhsT=w13[:, e * HP + h, w, 2 * P * kt : 2 * P * (kt + 1)].bitcast(FP4X4),
+                            lhsT_scale=w13s[:, e * HP + h, w, P * kt : P * (kt + 1)],
+                            rhs=c[:, r].bitcast(FP8X4),
+                            rhs_scale=z[:, r],
+                            start=(h == 0 and w == 0),
+                            stop=(h == HP - 1 and w == 1),
+                        )
+            nc.scalar.copy(dxs[e][:, :, P * a : P * (a + 1)], b[:])
+
+        def scatter(e, kt):
+            nc.vector.tensor_copy(
+                outs[kt][:].indirect(offsets[:, C // 16 * e : C // 16 * (e + 1)]), dxs[e][:, kt, :]
+            )
+
+        for s in range(NP - 1):
+            for t in range(4):
+                gather(s, t, None)
+                if t == 1 and s > 0:
+                    quant_g(s - 1, None)
+                    mm1(s - 1, 0)
+                    mm1(s - 1, 1)
+            interleave(s, None)
+        s = NP - 1
+        for t in range(4):
+            gather(s, t, 0)
+            if t == 2:
+                quant_g(s - 1, None)
+                mm1(s - 1, 0)
+                mm1(s - 1, 1)
+        for h in range(HP):
+            masks(h, 0, 0)
+        interleave(s, 0, 0)
+        interleave(s, 0, 1)
+        gather(s, 0, 1)
+        quant_g(s, 0, 0)
+        mm1(s, 0, (0,))
+        gather(s, 1, 1)
+        quant_g(s, 0, 1)
+        mm1(s, 0, (1,))
+        gather(s, 2, 1)
+        gather(s, 3, 1)
+        turn(0, 0, 0)
+        turn(0, 0, 1)
+        turn(0, 1, 0)
+        interleave(s, 1, 0)
+        turn(0, 1, 1)
+        interleave(s, 1, 1)
+        for h in range(HP):
+            masks(h, 0, 1)
+        products(0, 0, 0)
+        products(0, 0, 1)
+        quant_g(s, 1, 0)
+        mm1(s, 1, (0,))
+        products(0, 1, 0)
+        quant_g(s, 1, 1)
+        mm1(s, 1, (1,))
+        for a in range(AT):
+            for h in range(HP):
+                turn(1, a, h)
+        for a in range(AT):
+            for h in range(HP):
+                masks(h, 1, a)
+        masked(0, 0)
+        products(0, 1, 1)
+        quant_d(0, 0)
+        mm2(0, 0)
+        products(1, 0, 0)
+        masked(0, 1)
+        products(1, 0, 1)
+        quant_d(0, 1)
+        mm2(0, 1)
+        products(1, 1, 0)
+        masked(1, 0)
+        products(1, 1, 1)
+        quant_d(1, 0)
+        mm2(1, 0)
+        masked(1, 1)
+        scatter(0, 0)
+        quant_d(1, 1)
+        mm2(1, 1)
+        scatter(0, 1)
+        scatter(0, 2)
+        for kt in range(KT):
+            scatter(1, kt)
+            nc.sync.dma_start(out[P * kt : P * (kt + 1), :], outs[kt][:])

@@ -33,7 +33,7 @@ def tile_moe_bdx_glu_relu_kernel(
     nc = tc.nc
     with ExitStack() as ctx:
         keep = ctx.enter_context(tc.tile_pool(name="keep", bufs=1))
-        dypool = ctx.enter_context(tc.tile_pool(name="dypool", bufs=10))
+        dypool = ctx.enter_context(tc.tile_pool(name="dypool", bufs=4 * NP))
         gpool = ctx.enter_context(tc.tile_pool(name="gpool", bufs=2))
         dpool = ctx.enter_context(tc.tile_pool(name="dpool", bufs=3))
         psum = ctx.enter_context(tc.psum_pool(name="psum", bufs=1))
@@ -74,28 +74,31 @@ def tile_moe_bdx_glu_relu_kernel(
             nc.sync.dma_start(w[:].bitcast(I32), w2_words.bitcast(I32).rearrange("e s p w -> s p e w")[s])
             w2t.append(w)
 
-        def load_a(e, h):
-            j = slice(C * e, C * (e + 1))
+        def load_a1(e, h):
             t1 = keep.tile([P, 4, C], F32, name=f"a1t{e}{h}")
-            nc.sync.dma_start(t1[:], a1_rows[h][:, :, j])
+            nc.sync.dma_start(t1[:], a1_rows[h][:, :, C * e : C * (e + 1)])
             a1t[e, h] = t1
+
+        def load_a3(e, h):
             t3 = keep.tile([P, 2, 4, C], F32, name=f"mr{e}{h}")
-            nc.sync.dma_start(t3[:, 0], a3_rows[h][:, :, j])
+            nc.sync.dma_start(t3[:, 0], a3_rows[h][:, :, C * e : C * (e + 1)])
             mr[e, h] = t3
 
         load_dy(0)
+        load_a1(0, 0)
+        load_dy(1)
+        load_a1(0, 1)
         load_w2(0)
         w2s_rows = w2_scales.bitcast(I32).rearrange("e s f i -> f (e s) i")
         for q in range(4):
             nc.sync.dma_start(w2s[32 * q : 32 * q + 4].bitcast(I32), w2s_rows[4 * q : 4 * q + 4])
-        load_dy(1)
-        load_w2(1)
         load_dy(2)
-        load_w2(2)
-        load_a(0, 0)
-        load_a(0, 1)
+        load_w2(1)
         load_dy(3)
+        load_w2(2)
         load_w2(3)
+        load_a3(0, 0)
+        load_a3(0, 1)
         w13 = keep.tile([P, E * HP, 2, 2 * K], U8, name="w13", align_bytes=64)
         for w, words in ((0, w1_words), (1, w3_words)):
             nc.sync.dma_start(
@@ -106,8 +109,10 @@ def tile_moe_bdx_glu_relu_kernel(
             for q in range(4):
                 nc.sync.dma_start(w13s[32 * q : 32 * q + 4, :, w].bitcast(I32), rows[4 * q : 4 * q + 4])
 
-        load_a(1, 0)
-        load_a(1, 1)
+        load_a1(1, 0)
+        load_a1(1, 1)
+        load_a3(1, 0)
+        load_a3(1, 1)
 
         mask = keep.tile([P, HP, S, 4], BF16, name="mask")
 
@@ -129,28 +134,28 @@ def tile_moe_bdx_glu_relu_kernel(
             gs.append(z)
 
         g4 = {}
-        gb = {}
 
-        def gather(s, t, e):
-            if (s, e) not in g4:
-                n = S if e is None else C
-                g = gpool.tile([P, 4, n], F32, name="g4" if e is None else "g4e")
-                g4[s, e] = g
-            g = g4[s, e]
-            o = offsets[:] if e is None else offsets[:, C // 16 * e : C // 16 * (e + 1)]
-            j = gates[:] if e is None else gates[:, C * e : C * (e + 1)]
-            nc.vector.tensor_tensor(g[:, t, :], dy[s, t][:].indirect(o), j, MULT)
+        def gather(s, t, lo, hi, weights):
+            if (s, lo) not in g4:
+                g = gpool.tile([P, 4, hi - lo], F32, name=f"g4_{hi - lo}")
+                g4[s, lo] = g
+            nc.vector.tensor_tensor(
+                g4[s, lo][:, t, :], dy[s, t][:].indirect(offsets[:, lo // 16 : hi // 16]), weights, MULT
+            )
 
-        def interleave(s, e, a=0):
-            n = S if e is None else P
-            b = gpool.tile([P, n, 4], BF16, name="gb" if e is None else "gbe", align_bytes=64)
-            nc.scalar.copy(b[:], g4[s, e][:, :, n * a : n * (a + 1)].rearrange("p t j -> p j t"))
-            gb[s, e, a] = b
+        def new_gb(width, tag, bufs):
+            return gpool.tile([P, width, 4], BF16, name=tag, bufs=bufs, align_bytes=64)
 
-        def quant_g(s, e, a=0):
-            j = slice(0, S) if e is None else slice(C * e + P * a, C * e + P * (a + 1))
+        def interleave(b, s, base, lo, hi, first):
+            nc.scalar.copy(
+                b[:, lo - first : hi - first], g4[s, base][:, :, lo - base : hi - base].rearrange("p t j -> p j t")
+            )
+
+        def quant_g(b, s, lo, hi, first):
             nc.vector.quantize_mx(
-                out=gc[s][:, j].bitcast(FP8X4), scales=gs[s][:, j], in_=gb[s, e, a][:].rearrange("p j t -> p (j t)")
+                out=gc[s][:, lo:hi].bitcast(FP8X4),
+                scales=gs[s][:, lo:hi],
+                in_=b[:, lo - first : hi - first].rearrange("p j t -> p (j t)"),
             )
 
         bank = {}
@@ -237,54 +242,65 @@ def tile_moe_bdx_glu_relu_kernel(
                 outs[kt][:].indirect(offsets[:, C // 16 * e : C // 16 * (e + 1)]), dxs[e][:, kt, :]
             )
 
-        for s in range(NP - 1):
+        gx = gpool.tile([P, C], F32, name="gx", bufs=1)
+        nc.scalar.copy(gx[:], gates[:, 0:C])
+        gb = {}
+        for s in range(3):
             for t in range(4):
-                gather(s, t, None)
-                if t == 1 and s > 0:
-                    quant_g(s - 1, None)
+                gather(s, t, 0, S, gates[:])
+                if t == 2 and s > 0:
+                    quant_g(gb[s - 1], s - 1, 0, S, 0)
                     mm1(s - 1, 0)
                     mm1(s - 1, 1)
-            interleave(s, None)
-        s = NP - 1
+            if s < 2:
+                gb[s] = new_gb(S, "gb", 2)
+                interleave(gb[s], s, 0, 0, S, 0)
+                masks(s, 0, 0)
+                masks(s, 0, 1)
+        b2 = new_gb(C, "gb2", 1)
+        interleave(b2, 2, 0, 0, C, 0)
         for t in range(4):
-            gather(s, t, 0)
+            gather(3, t, 0, C, gx[:])
             if t == 2:
-                quant_g(s - 1, None)
-                mm1(s - 1, 0)
-                mm1(s - 1, 1)
-        for h in range(HP):
-            masks(h, 0, 0)
-        interleave(s, 0, 0)
-        interleave(s, 0, 1)
-        gather(s, 0, 1)
-        quant_g(s, 0, 0)
-        mm1(s, 0, (0,))
-        gather(s, 1, 1)
-        quant_g(s, 0, 1)
-        mm1(s, 0, (1,))
-        gather(s, 2, 1)
-        gather(s, 3, 1)
+                quant_g(b2, 2, 0, C, 0)
+                mm1(2, 0)
+        b3 = new_gb(C, "gb3", 1)
+        for a in range(AT):
+            interleave(b3, 3, 0, P * a, P * (a + 1), 0)
+        gx = gpool.tile([P, C], F32, name="gx", bufs=1)
+        nc.vector.tensor_copy(gx[:], gates[:, C:S])
+        gather(3, 0, C, S, gx[:])
+        quant_g(b3, 3, 0, P, 0)
+        mm1(3, 0, (0,))
+        gather(3, 1, C, S, gx[:])
+        quant_g(b3, 3, P, C, 0)
+        mm1(3, 0, (1,))
+        b2 = new_gb(C, "gb3", 1)
+        interleave(b2, 2, 0, C, S, C)
+        gather(3, 2, C, S, gx[:])
         turn(0, 0, 0)
         turn(0, 0, 1)
+        gather(3, 3, C, S, gx[:])
+        quant_g(b2, 2, C, S, C)
+        mm1(2, 1)
         turn(0, 1, 0)
-        interleave(s, 1, 0)
         turn(0, 1, 1)
-        interleave(s, 1, 1)
-        for h in range(HP):
-            masks(h, 0, 1)
+        b3 = new_gb(C, "gb3", 1)
+        for a in range(AT):
+            interleave(b3, 3, C, C + P * a, C + P * (a + 1), C)
         products(0, 0, 0)
+        quant_g(b3, 3, C, C + P, C)
+        mm1(3, 1, (0,))
         products(0, 0, 1)
-        quant_g(s, 1, 0)
-        mm1(s, 1, (0,))
-        products(0, 1, 0)
-        quant_g(s, 1, 1)
-        mm1(s, 1, (1,))
+        quant_g(b3, 3, C + P, S, C)
+        mm1(3, 1, (1,))
         for a in range(AT):
             for h in range(HP):
                 turn(1, a, h)
         for a in range(AT):
             for h in range(HP):
                 masks(h, 1, a)
+        products(0, 1, 0)
         masked(0, 0)
         products(0, 1, 1)
         quant_d(0, 0)

@@ -89,16 +89,18 @@ def tile_moe_bdx_glu_relu_kernel(
         load_dy(1)
         load_a1(0, 1)
         load_w2(0)
+        load_dy(2)
         w2s_rows = w2_scales.bitcast(I32).rearrange("e s f i -> f (e s) i")
         for q in range(4):
             nc.sync.dma_start(w2s[32 * q : 32 * q + 4].bitcast(I32), w2s_rows[4 * q : 4 * q + 4])
-        load_dy(2)
         load_w2(1)
         load_dy(3)
         load_w2(2)
         load_w2(3)
         load_a3(0, 0)
         load_a3(0, 1)
+        load_a1(1, 0)
+        load_a1(1, 1)
         w13 = keep.tile([P, E * HP, 2, 2 * K], U8, name="w13", align_bytes=64)
         for w, words in ((0, w1_words), (1, w3_words)):
             nc.sync.dma_start(
@@ -109,8 +111,6 @@ def tile_moe_bdx_glu_relu_kernel(
             for q in range(4):
                 nc.sync.dma_start(w13s[32 * q : 32 * q + 4, :, w].bitcast(I32), rows[4 * q : 4 * q + 4])
 
-        load_a1(1, 0)
-        load_a1(1, 1)
         load_a3(1, 0)
         load_a3(1, 1)
 
@@ -245,18 +245,23 @@ def tile_moe_bdx_glu_relu_kernel(
         gx = gpool.tile([P, C], F32, name="gx", bufs=1)
         nc.scalar.copy(gx[:], gates[:, 0:C])
         gb = {}
-        for s in range(3):
+        gb = {}
+        for s in range(2):
             for t in range(4):
                 gather(s, t, 0, S, gates[:])
                 if t == 2 and s > 0:
                     quant_g(gb[s - 1], s - 1, 0, S, 0)
                     mm1(s - 1, 0)
                     mm1(s - 1, 1)
-            if s < 2:
-                gb[s] = new_gb(S, "gb", 2)
-                interleave(gb[s], s, 0, 0, S, 0)
-                masks(s, 0, 0)
-                masks(s, 0, 1)
+            gb[s] = new_gb(S, "gb", 2)
+            interleave(gb[s], s, 0, 0, S, 0)
+            masks(s, 0, 0)
+            masks(s, 0, 1)
+        for t in range(4):
+            gather(2, t, 0, C, gx[:])
+        quant_g(gb[1], 1, 0, S, 0)
+        mm1(1, 0)
+        mm1(1, 1)
         b2 = new_gb(C, "gb2", 1)
         interleave(b2, 2, 0, 0, C, 0)
         for t in range(4):
@@ -269,22 +274,26 @@ def tile_moe_bdx_glu_relu_kernel(
             interleave(b3, 3, 0, P * a, P * (a + 1), 0)
         gx = gpool.tile([P, C], F32, name="gx", bufs=1)
         nc.vector.tensor_copy(gx[:], gates[:, C:S])
-        gather(3, 0, C, S, gx[:])
+        gather(2, 0, C, S, gx[:])
+        gather(2, 1, C, S, gx[:])
         quant_g(b3, 3, 0, P, 0)
         mm1(3, 0, (0,))
-        gather(3, 1, C, S, gx[:])
         quant_g(b3, 3, P, C, 0)
         mm1(3, 0, (1,))
-        b2 = new_gb(C, "gb3", 1)
-        interleave(b2, 2, 0, C, S, C)
-        gather(3, 2, C, S, gx[:])
+        gather(2, 2, C, S, gx[:])
+        gather(2, 3, C, S, gx[:])
         turn(0, 0, 0)
         turn(0, 0, 1)
-        gather(3, 3, C, S, gx[:])
-        quant_g(b2, 2, C, S, C)
-        mm1(2, 1)
+        b2 = new_gb(C, "gb3", 1)
+        interleave(b2, 2, C, C, S, C)
+        gather(3, 0, C, S, gx[:])
+        gather(3, 1, C, S, gx[:])
         turn(0, 1, 0)
         turn(0, 1, 1)
+        gather(3, 2, C, S, gx[:])
+        quant_g(b2, 2, C, S, C)
+        mm1(2, 1)
+        gather(3, 3, C, S, gx[:])
         b3 = new_gb(C, "gb3", 1)
         for a in range(AT):
             interleave(b3, 3, C, C + P * a, C + P * (a + 1), C)

@@ -120,8 +120,8 @@ def tile_moe_bdx_glu_relu_kernel(
             j = slice(P * half, P * half + P)
             nc.scalar.activation(mr[e, h][:, 1, :, j], a1t[e, h][:, :, j], RELU)
             nc.scalar.activation(
-                mask[:, h, C * e + P * half : C * e + P * half + P],
-                mr[e, h][:, 1, :, j].rearrange("p t j -> p j t"),
+                mask[:, h, C * e + P * half : C * e + P * half + P].rearrange("p (c i) t -> p c t i", i=4),
+                mr[e, h][:, 1, :, j].rearrange("p t (c i) -> p c t i", i=4),
                 SIGN,
             )
 
@@ -148,7 +148,8 @@ def tile_moe_bdx_glu_relu_kernel(
 
         def interleave(b, s, base, lo, hi, first):
             nc.scalar.copy(
-                b[:, lo - first : hi - first], g4[s, base][:, :, lo - base : hi - base].rearrange("p t j -> p j t")
+                b[:, lo - first : hi - first].rearrange("p (c i) t -> p c t i", i=4),
+                g4[s, base][:, :, lo - base : hi - base].rearrange("p t (c i) -> p c t i", i=4),
             )
 
         def quant_g(b, s, lo, hi, first):

from contextlib import ExitStack

import concourse.mybir as mybir
from concourse.masks import make_identity

E, C, T, K, H, N = 2, 256, 640, 384, 1024, 2048
S = E * C
P = 128
NP = N // 512
HP = H // 512
KT = K // P
AT = C // P

FLOPS = 2 * S * N * H + 2 * 2 * S * H * K
BYTES = 4 * (N * T + 2 * H * S + P * S + K * T) + E * (N * H + 2 * H * K) * 17 // 32 + 2 * S * 8

F32 = mybir.dt.float32
BF16 = mybir.dt.bfloat16
I32 = mybir.dt.int32
U32 = mybir.dt.uint32
U16 = mybir.dt.uint16
U8 = mybir.dt.uint8
FP8X4 = mybir.dt.float8_e4m3fn_x4
FP4X4 = mybir.dt.float4_e2m1fn_x4
MULT = mybir.AluOpType.mult
RELU = mybir.ActivationFunctionType.Relu
SIGN = mybir.ActivationFunctionType.Sign


def tile_moe_bdx_glu_relu_kernel(
    tc, dyT, a1, a3, w2_words, w2_scales, w1_words, w1_scales, w3_words, w3_scales, gate, offs, out
):
    nc = tc.nc
    with ExitStack() as ctx:
        keep = ctx.enter_context(tc.tile_pool(name="keep", bufs=1))
        dypool = ctx.enter_context(tc.tile_pool(name="dypool", bufs=4 * NP))
        gpool = ctx.enter_context(tc.tile_pool(name="gpool", bufs=2))
        dpool = ctx.enter_context(tc.tile_pool(name="dpool", bufs=3))
        psum = ctx.enter_context(tc.psum_pool(name="psum", bufs=1))

        offsets = keep.tile([P, S // 16], U16, name="offsets")
        nc.sync.dma_start(offsets[:], offs)
        gates = keep.tile([P, S], F32, name="gates")
        nc.scalar.dma_start(gates[:], gate[0:P, :])

        w2s = keep.tile([P, E * NP, H], U8, name="w2s", align_bytes=64)
        nc.vector.memset(w2s[:].bitcast(I32), 0)
        w13s = keep.tile([P, E * HP, 2, K], U8, name="w13s", align_bytes=64)
        nc.vector.memset(w13s[:].bitcast(I32), 0)
        ident = keep.tile([P, P], F32, name="ident")
        make_identity(nc, ident[:])
        outs = []
        for kt in range(KT):
            o = keep.tile([P, T], F32, name=f"out{kt}")
            nc.gpsimd.memset(o[:], 0.0)
            outs.append(o)

        dy_rows = dyT.rearrange("(s p t) w -> s t p w", s=NP, p=P, t=4)
        a1_rows = a1.rearrange("(s p t) j -> s p t j", s=HP, p=P, t=4)
        a3_rows = a3.rearrange("(s p t) j -> s p t j", s=HP, p=P, t=4)
        dy = {}
        w2t = []
        a1t = {}
        mr = {}

        def load_dy(s):
            for t in range(4):
                d = dypool.tile([P, T], F32, name="dy")
                nc.sync.dma_start(d[:], dy_rows[s, t])
                dy[s, t] = d

        def load_w2(s):
            w = keep.tile([P, E, 2 * H], U8, name=f"w2t{s}", align_bytes=64)
            nc.sync.dma_start(w[:].bitcast(I32), w2_words.bitcast(I32).rearrange("e s p w -> s p e w")[s])
            w2t.append(w)

        def load_a1(e, h):
            t1 = keep.tile([P, 4, C], F32, name=f"a1t{e}{h}")
            nc.sync.dma_start(t1[:], a1_rows[h][:, :, C * e : C * (e + 1)])
            a1t[e, h] = t1

        def load_a3(e, h):
            t3 = keep.tile([P, 2, 4, C], F32, name=f"mr{e}{h}")
            nc.sync.dma_start(t3[:, 0], a3_rows[h][:, :, C * e : C * (e + 1)])
            mr[e, h] = t3

        load_dy(0)
        load_a1(0, 0)
        load_dy(1)
        load_a1(0, 1)
        load_w2(0)
        load_dy(2)
        w2s_rows = w2_scales.bitcast(I32).rearrange("e s f i -> f (e s) i")
        for q in range(4):
            nc.sync.dma_start(w2s[32 * q : 32 * q + 4].bitcast(I32), w2s_rows[4 * q : 4 * q + 4])
        load_w2(1)
        load_dy(3)
        load_w2(2)
        load_w2(3)
        load_a3(0, 0)
        load_a3(0, 1)
        load_a1(1, 0)
        load_a1(1, 1)
        w13 = keep.tile([P, E * HP, 2, 2 * K], U8, name="w13", align_bytes=64)
        for w, words in ((0, w1_words), (1, w3_words)):
            nc.sync.dma_start(
                w13[:, :, w].bitcast(I32), words.bitcast(I32).rearrange("e s p w -> p (e s) w")
            )
        for w, scales in ((0, w1_scales), (1, w3_scales)):
            rows = scales.bitcast(I32).rearrange("e s f k -> f (e s) k")
            for q in range(4):
                nc.sync.dma_start(w13s[32 * q : 32 * q + 4, :, w].bitcast(I32), rows[4 * q : 4 * q + 4])

        load_a3(1, 0)
        load_a3(1, 1)

        mask = keep.tile([P, HP, S, 4], BF16, name="mask")

        def masks(h, e, half):
            j = slice(P * half, P * half + P)
            nc.scalar.activation(mr[e, h][:, 1, :, j], a1t[e, h][:, :, j], RELU)
            nc.scalar.activation(
                mask[:, h, C * e + P * half : C * e + P * half + P].rearrange("p (c i) t -> p c t i", i=4),
                mr[e, h][:, 1, :, j].rearrange("p t (c i) -> p c t i", i=4),
                SIGN,
            )

        gc = []
        gs = []
        for s in range(NP):
            c = keep.tile([P, S], U32, name=f"gc{s}", align_bytes=64)
            z = keep.tile([P, S], U8, name=f"gs{s}", align_bytes=64)
            gc.append(c)
            gs.append(z)

        g4 = {}

        def gather(s, t, lo, hi, weights):
            if (s, lo) not in g4:
                g = gpool.tile([P, 4, hi - lo], F32, name=f"g4_{hi - lo}")
                g4[s, lo] = g
            nc.vector.tensor_tensor(
                g4[s, lo][:, t, :], dy[s, t][:].indirect(offsets[:, lo // 16 : hi // 16]), weights, MULT
            )

        def new_gb(width, tag, bufs):
            return gpool.tile([P, width, 4], BF16, name=tag, bufs=bufs, align_bytes=64)

        def interleave(b, s, base, lo, hi, first):
            nc.scalar.copy(
                b[:, lo - first : hi - first].rearrange("p (c i) t -> p c t i", i=4),
                g4[s, base][:, :, lo - base : hi - base].rearrange("p t (c i) -> p c t i", i=4),
            )

        def quant_g(b, s, lo, hi, first):
            nc.vector.quantize_mx(
                out=gc[s][:, lo:hi].bitcast(FP8X4),
                scales=gs[s][:, lo:hi],
                in_=b[:, lo - first : hi - first].rearrange("p j t -> p (j t)"),
            )

        bank = {}

        def mm1(s, e, some=range(AT)):
            for a in some:
                j = slice(C * e + P * a, C * e + P * a + P)
                for h in range(HP):
                    if s == 0:
                        b = psum.tile([P, 512], F32, name=f"bank{e}{a}{h}")
                        bank[e, a, h] = b
                    nc.tensor.matmul_mx(
                        out=bank[e, a, h][:],
                        lhsT=gc[s][:, j].bitcast(FP8X4),
                        lhsT_scale=gs[s][:, j],
                        rhs=w2t[s][:, e, 1024 * h : 1024 * (h + 1)].bitcast(FP4X4),
                        rhs_scale=w2s[:, e * NP + s, 512 * h : 512 * (h + 1)],
                        start=(s == 0),
                        stop=(s == NP - 1),
                    )

        def turn(e, a, h):
            d = dpool.tile([P, 4, P], F32, name="dhs")
            nc.scalar.copy(d[:], bank[e, a, h][:].rearrange("p (m t) -> p t m", t=4))
            b = psum.tile([P, 4, P], F32, name=f"bank{e}{a}{h}")
            for t in range(4):
                nc.tensor.transpose(b[:, t, :], d[:, t, :], ident[:])
            bank[e, a, h] = b

        dq = {}

        def products(e, a, h):
            if h == 0:
                q = dpool.tile([P, HP, 2, P, 4], BF16, name="dq", align_bytes=64)
                dq[e, a] = q
            j = slice(P * a, P * a + P)
            nc.vector.tensor_tensor(
                dq[e, a][:, h],
                bank[e, a, h][:].rearrange("p t j -> p j t").unsqueeze(1).to_broadcast([P, 2, P, 4]),
                mr[e, h][:, :, :, j].rearrange("p w t j -> p w j t"),
                MULT,
            )

        def masked(e, a):
            j = slice(C * e + P * a, C * e + P * a + P)
            m = dq[e, a][:, :, 0]
            nc.vector.tensor_tensor(m, m, mask[:, :, j], MULT)

        dc = {}

        def quant_d(e, a):
            c = dpool.tile([P, HP * 2 * P], U32, name="dc", align_bytes=64)
            z = dpool.tile([P, HP * 2 * P], U8, name="ds", align_bytes=64)
            nc.vector.quantize_mx(
                out=c[:].bitcast(FP8X4), scales=z[:], in_=dq[e, a][:].rearrange("p h w j t -> p (h w j t)")
            )
            dc[e, a] = (c, z)

        dxs = []
        for e in range(E):
            d = keep.tile([P, KT, C], F32, name=f"dxs{e}")
            dxs.append(d)

        def mm2(e, a):
            c, z = dc[e, a]
            b = psum.tile([P, KT, P], F32, name=f"bank{e}{a}0")
            for kt in range(KT):
                for h in range(HP):
                    for w in range(2):
                        r = slice(P * (2 * h + w), P * (2 * h + w + 1))
                        nc.tensor.matmul_mx(
                            out=b[:, kt],
                            lhsT=w13[:, e * HP + h, w, 2 * P * kt : 2 * P * (kt + 1)].bitcast(FP4X4),
                            lhsT_scale=w13s[:, e * HP + h, w, P * kt : P * (kt + 1)],
                            rhs=c[:, r].bitcast(FP8X4),
                            rhs_scale=z[:, r],
                            start=(h == 0 and w == 0),
                            stop=(h == HP - 1 and w == 1),
                        )
            nc.scalar.copy(dxs[e][:, :, P * a : P * (a + 1)], b[:])

        def scatter(e, kt):
            nc.vector.tensor_copy(
                outs[kt][:].indirect(offsets[:, C // 16 * e : C // 16 * (e + 1)]), dxs[e][:, kt, :]
            )

        gx = gpool.tile([P, C], F32, name="gx", bufs=1)
        nc.scalar.copy(gx[:], gates[:, 0:C])
        gb = {}
        gb = {}
        for s in range(2):
            for t in range(4):
                gather(s, t, 0, S, gates[:])
                if t == 2 and s > 0:
                    quant_g(gb[s - 1], s - 1, 0, S, 0)
                    mm1(s - 1, 0)
                    mm1(s - 1, 1)
            gb[s] = new_gb(S, "gb", 2)
            interleave(gb[s], s, 0, 0, S, 0)
            masks(s, 0, 0)
            masks(s, 0, 1)
        for t in range(4):
            gather(2, t, 0, C, gx[:])
        quant_g(gb[1], 1, 0, S, 0)
        mm1(1, 0)
        mm1(1, 1)
        b2 = new_gb(C, "gb2", 1)
        interleave(b2, 2, 0, 0, C, 0)
        for t in range(4):
            gather(3, t, 0, C, gx[:])
            if t == 2:
                quant_g(b2, 2, 0, C, 0)
                mm1(2, 0)
        b3 = new_gb(C, "gb3", 1)
        for a in range(AT):
            interleave(b3, 3, 0, P * a, P * (a + 1), 0)
        gx = gpool.tile([P, C], F32, name="gx", bufs=1)
        nc.vector.tensor_copy(gx[:], gates[:, C:S])
        gather(2, 0, C, S, gx[:])
        gather(2, 1, C, S, gx[:])
        quant_g(b3, 3, 0, P, 0)
        mm1(3, 0, (0,))
        quant_g(b3, 3, P, C, 0)
        mm1(3, 0, (1,))
        gather(2, 2, C, S, gx[:])
        gather(2, 3, C, S, gx[:])
        turn(0, 0, 0)
        turn(0, 0, 1)
        b2 = new_gb(C, "gb3", 1)
        interleave(b2, 2, C, C, S, C)
        gather(3, 0, C, S, gx[:])
        gather(3, 1, C, S, gx[:])
        turn(0, 1, 0)
        turn(0, 1, 1)
        gather(3, 2, C, S, gx[:])
        quant_g(b2, 2, C, S, C)
        mm1(2, 1)
        gather(3, 3, C, S, gx[:])
        b3 = new_gb(C, "gb3", 1)
        for a in range(AT):
            interleave(b3, 3, C, C + P * a, C + P * (a + 1), C)
        products(0, 0, 0)
        quant_g(b3, 3, C, C + P, C)
        mm1(3, 1, (0,))
        products(0, 0, 1)
        quant_g(b3, 3, C + P, S, C)
        mm1(3, 1, (1,))
        for a in range(AT):
            for h in range(HP):
                turn(1, a, h)
        for a in range(AT):
            for h in range(HP):
                masks(h, 1, a)
        products(0, 1, 0)
        masked(0, 0)
        products(0, 1, 1)
        quant_d(0, 0)
        mm2(0, 0)
        products(1, 0, 0)
        masked(0, 1)
        products(1, 0, 1)
        quant_d(0, 1)
        mm2(0, 1)
        products(1, 1, 0)
        masked(1, 0)
        products(1, 1, 1)
        quant_d(1, 0)
        mm2(1, 0)
        masked(1, 1)
        scatter(0, 0)
        quant_d(1, 1)
        mm2(1, 1)
        scatter(0, 1)
        scatter(0, 2)
        for kt in range(KT):
            scatter(1, kt)
            nc.sync.dma_start(out[P * kt : P * (kt + 1), :], outs[kt][:])
